import numpy as np
import ml_dtypes


def mxq(x, axis, fmt="e4m3"):
    dtype, down = {"e4m3": (ml_dtypes.float8_e4m3fn, 7), "e5m2": (ml_dtypes.float8_e5m2, 14)}[fmt]
    v = np.moveaxis(np.asarray(x, np.float32).astype(ml_dtypes.bfloat16).astype(np.float64), axis, -1)
    blocks = v.reshape(v.shape[:-1] + (-1, 32))
    amax = np.abs(blocks).max(-1, keepdims=True)
    byte = np.maximum(np.where(amax > 0, np.frexp(amax)[1] - 1 + 127, 0) - down, 1)
    scale = np.exp2(byte - 127.0)
    codes = (blocks / scale).astype(np.float32).astype(dtype).astype(np.float64)
    return np.moveaxis((codes * scale).reshape(v.shape), -1, axis)


WIDE = False


def mx_kscale(k):
    if not WIDE:
        return np.ones(k)
    levels = np.array([10, -10, 5, -5, 0])
    if k % 512:
        return np.exp2(np.random.permutation(np.resize(levels, k // 32))).repeat(32)
    a = np.empty((k // 512, 16))
    for p in range(k // 512):
        a[p, :8] = np.random.permutation(np.resize(levels, 8))
        for g in range(8):
            far = levels[np.abs(levels - a[p, g]) >= 10]
            a[p, g + 8] = far[np.random.randint(len(far))]
    return np.exp2(a.ravel()).repeat(32)


def f64(x):
    return np.asarray(x).astype(np.float64)


def striped(idx):
    return np.tile(idx.reshape(-1, 16).T, (8, 1)).astype(np.uint16)


def unstriped(offs):
    return offs[:16].T.reshape(-1).astype(np.int64)


def pack_weight(w):
    k, n = w.shape
    w = f64(np.asarray(w, np.float32).astype(ml_dtypes.bfloat16)).reshape(k // 32, 32, n)
    amax = np.abs(w).max(1)
    byte = np.clip(np.where(amax > 0, np.frexp(amax)[1] - 1 + 127 - 7, 1), 1, 254)
    scaled = (w * np.exp2(127.0 - byte)[:, None, :]).reshape(k, n).astype(np.float32)
    words = np.ascontiguousarray(scaled.reshape(k // 512, 128, 4, n).transpose(0, 1, 3, 2)).astype(ml_dtypes.float8_e4m3fn).view(np.uint8)
    return words, np.ascontiguousarray(byte.astype(np.uint8).reshape(k // 512, 16, n))


def unpack_weight(words, scales):
    g, p, n, _ = words.shape
    vals = np.ascontiguousarray(words).view(ml_dtypes.float8_e4m3fn).astype(np.float64) * np.repeat(np.exp2(scales.astype(np.float64) - 127.0), 8, axis=1)[..., None]
    return vals.transpose(0, 1, 3, 2).reshape(g * 512, n)


def silu(v):
    return v / (1.0 + np.exp(-np.maximum(v, -700.0)))


K, T, S, V, N = 1024, 2048, 1024, 512, 128


def setup_inputs():
    n = np.random.standard_normal
    s = mx_kscale(K)[:, None]
    packed_w1 = pack_weight(n((K, N)) / np.sqrt(K) / s)
    packed_w2 = pack_weight(n((K, N)) / np.sqrt(K) / s)
    packed_w3 = pack_weight(n((K, N)) / np.sqrt(K) / s)
    return {
        "xT": (n((K, T)) * s).astype(np.float32),
        "w1_words": packed_w1[0],
        "w1_scales": packed_w1[1],
        "w2_words": packed_w2[0],
        "w2_scales": packed_w2[1],
        "w3_words": packed_w3[0],
        "w3_scales": packed_w3[1],
        "offs": striped(np.random.permutation(T)[:S]),
        "cen": striped(np.random.permutation(S)[:V]),
        "pos1": striped(np.random.permutation(S)[:V]),
        "pos2": striped(np.random.permutation(S)[:V]),
        "pos3": striped(np.random.permutation(S)[:V]),
    }


def reference(xT, w1_words, w1_scales, w2_words, w2_scales, w3_words, w3_scales, offs, cen, pos1, pos2, pos3):
    xq = mxq(f64(xT)[:, unstriped(offs)], 0, "e4m3")
    h = unpack_weight(w3_words, w3_scales).T @ xq
    g = unpack_weight(w1_words, w1_scales).T @ xq
    gc = g[:, unstriped(cen)]
    s = unpack_weight(w2_words, w2_scales).T @ xq
    sc = s[:, unstriped(cen)]
    return silu(h[:, unstriped(pos1)] * gc + sc) + silu(h[:, unstriped(pos2)] * gc + sc) + silu(h[:, unstriped(pos3)] * gc + sc)

@@ -1,0 +1,236 @@
+from contextlib import ExitStack
+
+import concourse.mybir as mybir
+from concourse.masks import make_identity
+
+K, T, S, V, N = 1024, 2048, 1024, 512, 128
+FLOPS = 3 * 2 * K * N * S
+
+F32 = mybir.dt.float32
+BF16 = mybir.dt.bfloat16
+I32 = mybir.dt.int32
+U32 = mybir.dt.uint32
+U16 = mybir.dt.uint16
+U8 = mybir.dt.uint8
+FP8X4 = mybir.dt.float8_e4m3fn_x4
+SILU = mybir.ActivationFunctionType.Silu
+MULT = mybir.AluOpType.mult
+ADD = mybir.AluOpType.add
+
+P = 128
+PASSES = 2
+HALF = 512
+QUARTER = 256
+WIDE = 384
+
+PIECES = [
+    [(1024, 1024, 0), (0, 1024, 688)],
+    [(1024, 1024, 0), (0, 1024, 688)],
+    [(1024, 1024, 0), (0, 1024, 496)],
+    [(1536, 512, 0), (1024, 512, 0), (512, 512, 0), (0, 256, 256), (256, 256, 176)],
+]
+LAP = 8
+
+
+def tile_picked_filmg_silu_e_kernel(
+    tc, xT, w1_words, w1_scales, w2_words, w2_scales, w3_words, w3_scales, offs, cen, pos1, pos2, pos3, out
+):
+    nc = tc.nc
+    with ExitStack() as ctx:
+        keep = ctx.enter_context(tc.tile_pool(name="keep", bufs=1))
+        psum = ctx.enter_context(tc.psum_pool(name="psum", bufs=1))
+
+        def load_list(src, name):
+            t = keep.tile(list(src.shape), U16, name=name)
+            nc.sync.dma_start(t[:], src)
+            return t
+
+        def bank(i):
+            return psum.tile([P, HALF], F32, name="bank%d" % i, tag="bank%d" % i)
+
+        offs_t = load_list(offs, "offs_t")
+
+        w_words = [w1_words, w2_words, w3_words]
+        w_scales = [w1_scales, w2_scales, w3_scales]
+
+        wsc = keep.tile([P, 3, PASSES, N], U8, name="wsc", align_bytes=64)
+        wsc_i = wsc[:].bitcast(I32)
+        nc.vector.memset(wsc_i, 0)
+
+        def load_scales(first, count):
+            for n in range(first, first + count):
+                i, q = divmod(n, 4)
+                nc.sync.dma_start(
+                    wsc_i[32 * q : 32 * q + 4, i],
+                    w_scales[i][:, 4 * q : 4 * q + 4, :].rearrange("z r c -> r z c").bitcast(I32),
+                )
+
+        zero_in = keep.tile([P, 1], F32, name="zero_in")
+        zero = keep.tile([P, 1], F32, name="zero")
+        nc.vector.memset(zero_in[:], 0.0)
+        nc.scalar.activation(zero[:], zero_in[:], SILU)
+
+        ident = keep.tile([P, P], F32, name="ident")
+        make_identity(nc, ident[:])
+
+        x4 = xT.rearrange("(z p j) t -> z p j t", z=PASSES, j=4)
+        raw = [keep.tile([P, 2 * T], F32, name="raw%d" % a)[:].rearrange("p (u t) -> p u t", u=2) for a in range(4)]
+        big = keep.tile([P, 5 * T], U32, name="big", align_bytes=64)
+        starts = [0, T - LAP, 3 * T - LAP, 4 * T - 2 * LAP]
+        pairs = [big[:, st : st + T] for st in starts]
+        picked = [keep.tile([P, 2 * S], U32, name="picked%d" % z)[:].rearrange("p (u e) -> p u e", u=2) for z in range(PASSES)]
+        woven1 = keep.tile([P, 2 * S], U32, name="woven1", align_bytes=64)
+        woven = [w.rearrange("p (e u) -> p e u", u=2) for w in (big[:, 2 * T : 3 * T], woven1[:])]
+        codes = [keep.tile([P, S], U32, name="codes%d" % z, align_bytes=64) for z in range(PASSES)]
+        xsc = [keep.tile([P, S], U8, name="xsc%d" % z, align_bytes=64) for z in range(PASSES)]
+
+        for a in range(4):
+            z, u = divmod(a, 2)
+            for c0, width, share in PIECES[a]:
+                nc.sync.dma_start(raw[a][:, :, c0 : c0 + width], x4[z][:, 2 * u : 2 * u + 2, c0 : c0 + width])
+            if a < 2:
+                load_scales(6 * a, 6)
+
+        wt = []
+        for i in range(3):
+            t = keep.tile([P, PASSES, N], U32, name="wt%d" % i, align_bytes=64)
+            nc.sync.dma_start(t[:].bitcast(I32), w_words[i].rearrange("z p n t -> p z (n t)").bitcast(I32))
+            wt.append(t)
+        cen_t = load_list(cen, "cen_t")
+        pos_t = [load_list(src, "pos%d_t" % d) for d, src in enumerate((pos1, pos2, pos3))]
+
+        def cast(a, c0, c1, on_scalar):
+            dst = pairs[a][:, c0:c1].bitcast(BF16).rearrange("p (t u) -> p t u", u=2)
+            src = raw[a][:, :, c0:c1].rearrange("p u t -> p t u")
+            if on_scalar:
+                nc.scalar.copy(dst, src)
+            else:
+                nc.vector.tensor_copy(dst, src)
+
+        def cast_pair(a):
+            for c0, width, share in PIECES[a]:
+                if share > 0:
+                    cast(a, c0, c0 + share, False)
+                if share < width:
+                    cast(a, c0 + share, c0 + width, True)
+
+        def gather(a, e0, e1):
+            z, u = divmod(a, 2)
+            nc.vector.tensor_copy(picked[z][:, u, e0:e1], pairs[a].indirect(offs_t[:, e0 // 16 : e1 // 16]))
+
+        def weave(z, e0, e1, on_scalar):
+            src = picked[z][:, :, e0:e1].rearrange("p u e -> p e u")
+            dst = woven[z][:, e0:e1, :]
+            if on_scalar:
+                nc.scalar.copy(dst, src)
+            else:
+                nc.vector.tensor_copy(dst.bitcast(I32), picked[z][:, :, e0:e1].bitcast(I32).rearrange("p u e -> p e u"))
+
+        def quantize(z, e0, e1):
+            nc.vector.quantize_mx(
+                out=codes[z][:, e0:e1].bitcast(FP8X4),
+                scales=xsc[z][:, e0:e1],
+                in_=woven[z][:, e0:e1, :].rearrange("p e u -> p (e u)").bitcast(BF16),
+            )
+
+        acc = [[bank(2 * i + hf) for hf in range(2)] for i in range(3)]
+
+        def product(i, z, hf):
+            cols = slice(hf * HALF, (hf + 1) * HALF)
+            nc.tensor.matmul_mx(
+                out=acc[i][hf][:],
+                lhsT=wt[i][:, z, :].bitcast(FP8X4),
+                lhsT_scale=wsc[:, i, z, :],
+                rhs=codes[z][:, cols].bitcast(FP8X4),
+                rhs_scale=xsc[z][:, cols],
+                start=(z == 0),
+                stop=(z == PASSES - 1),
+            )
+
+        cast_pair(0)
+        gather(0, 0, S)
+        cast_pair(1)
+        gather(1, 0, HALF)
+        gather(1, HALF, S)
+        weave(0, 0, HALF, False)
+        weave(0, HALF, S, False)
+        quantize(0, 0, HALF)
+        quantize(0, HALF, S)
+        cast_pair(2)
+        gather(2, 0, S)
+        cast_pair(3)
+        for hf in range(2):
+            for i in range(3):
+                product(i, 0, hf)
+        nq = S // QUARTER
+        for q in range(nq + 2):
+            if q < nq:
+                gather(3, q * QUARTER, (q + 1) * QUARTER)
+                weave(1, q * QUARTER, (q + 1) * QUARTER, True)
+            if q >= 2:
+                quantize(1, (q - 2) * QUARTER, (q - 1) * QUARTER)
+        res = [keep.tile([P, S], F32, name="res%d" % i) for i in range(3)]
+        for hf in range(2):
+            for i in range(3):
+                product(i, 1, hf)
+        g_sb, s_sb, h_sb = res
+        nc.scalar.copy(g_sb[:, :HALF], acc[0][0][:])
+        nc.vector.tensor_copy(g_sb[:, HALF:], acc[0][1][:])
+        for hf in range(2):
+            for i in (1, 2):
+                nc.scalar.copy(res[i][:, hf * HALF : (hf + 1) * HALF], acc[i][hf][:])
+
+        gc_all = keep.tile([P, V], F32, name="gc_all")
+        sc_all = keep.tile([P, V], F32, name="sc_all")
+        nc.vector.tensor_copy(gc_all[:], g_sb[:].indirect(cen_t[:]))
+        nc.vector.tensor_copy(sc_all[:], s_sb[:].indirect(cen_t[:]))
+
+        def scaled(dst, d, v0, v1):
+            nc.vector.tensor_tensor(dst, h_sb[:].indirect(pos_t[d][:, v0 // 16 : v1 // 16]), gc_all[:, v0:v1], MULT)
+
+        sc = sc_all[:, :WIDE]
+        prod = keep.tile([P, 3, WIDE], F32, name="prod_a")
+        for d in range(3):
+            scaled(prod[:, d, :], d, 0, WIDE)
+        nblk = WIDE // P
+        act = keep.tile([P, 3, WIDE], F32, name="act_a", tag="act")
+        o_sb = keep.tile([P, WIDE], F32, name="o_a")
+        ob = [bank(b) for b in range(nblk)]
+        for d in range(3):
+            if d < 2:
+                whole = bank(6 + d)
+                ub = [whole[:, b * P : (b + 1) * P] for b in range(nblk)]
+            else:
+                ub = [bank(3 + b)[:, :P] for b in range(nblk)]
+            for b in range(nblk):
+                blk = slice(b * P, (b + 1) * P)
+                nc.tensor.matmul(ub[b], sc[:, blk], ident[:], start=True, stop=False, is_transpose=True)
+                nc.tensor.matmul(ub[b], prod[:, d, blk], ident[:], start=False, stop=True, is_transpose=True)
+                if d == 2:
+                    nc.scalar.activation(act[:, d, blk], ub[b], SILU, bias=zero[:])
+            if d < 2:
+                nc.scalar.activation(act[:, d, :], whole[:, :WIDE], SILU, bias=zero[:])
+            for b in range(nblk):
+                blk = slice(b * P, (b + 1) * P)
+                nc.tensor.matmul(ob[b][:, :P], act[:, d, blk], ident[:], start=(d == 0), stop=(d == 2), is_transpose=True)
+        for b in range(nblk):
+            nc.scalar.copy(o_sb[:, b * P : (b + 1) * P], ob[b][:, :P])
+        nc.sync.dma_start(out[:, :WIDE], o_sb[:])
+
+        rest = V - WIDE
+        sc = sc_all[:, WIDE:]
+        prod = keep.tile([P, 3, rest], F32, name="prod_b")
+        scaled(prod[:, 0, :], 0, WIDE, V)
+        scaled(prod[:, 1, :], 1, WIDE, V)
+        pre = keep.tile([P, 3, rest], F32, name="pre_b")
+        act = keep.tile([P, 3, rest], F32, name="act_b", tag="act")
+        two = keep.tile([P, rest], F32, name="two_b")
+        o_sb = keep.tile([P, rest], F32, name="o_b")
+        nc.vector.tensor_tensor(pre[:, 0:2, :], prod[:, 0:2, :], sc.unsqueeze(1).to_broadcast([P, 2, rest]), ADD)
+        nc.scalar.activation(act[:, 0:2, :], pre[:, 0:2, :], SILU, bias=zero[:])
+        scaled(prod[:, 2, :], 2, WIDE, V)
+        nc.vector.tensor_tensor(pre[:, 2, :], prod[:, 2, :], sc, ADD)
+        nc.scalar.activation(act[:, 2, :], pre[:, 2, :], SILU, bias=zero[:])
+        nc.vector.tensor_tensor(two[:], act[:, 0, :], act[:, 1, :], ADD)
+        nc.vector.tensor_tensor(o_sb[:], two[:], act[:, 2, :], ADD)
+        nc.sync.dma_start(out[:, WIDE:], o_sb[:])

@@ -24,7 +24,7 @@ QUARTER = 256
 WIDE = 384
 
 PIECES = [
-    [(1024, 1024, 0), (0, 1024, 688)],
+    [(0, 2048, 1376)],
     [(1024, 1024, 0), (0, 1024, 688)],
     [(1024, 1024, 0), (0, 1024, 496)],
     [(1536, 512, 0), (1024, 512, 0), (512, 512, 0), (0, 256, 256), (256, 256, 176)],
@@ -48,22 +48,12 @@ def tile_picked_filmg_silu_e_kernel(
         def bank(i):
             return psum.tile([P, HALF], F32, name="bank%d" % i, tag="bank%d" % i)
 
-        offs_t = load_list(offs, "offs_t")
-
         w_words = [w1_words, w2_words, w3_words]
         w_scales = [w1_scales, w2_scales, w3_scales]
 
         wsc = keep.tile([P, 3, PASSES, N], U8, name="wsc", align_bytes=64)
         wsc_i = wsc[:].bitcast(I32)
         nc.vector.memset(wsc_i, 0)
-
-        def load_scales(first, count):
-            for n in range(first, first + count):
-                i, q = divmod(n, 4)
-                nc.sync.dma_start(
-                    wsc_i[32 * q : 32 * q + 4, i],
-                    w_scales[i][:, 4 * q : 4 * q + 4, :].rearrange("z r c -> r z c").bitcast(I32),
-                )
 
         zero_in = keep.tile([P, 1], F32, name="zero_in")
         zero = keep.tile([P, 1], F32, name="zero")
@@ -88,14 +78,18 @@ def tile_picked_filmg_silu_e_kernel(
             z, u = divmod(a, 2)
             for c0, width, share in PIECES[a]:
                 nc.sync.dma_start(raw[a][:, :, c0 : c0 + width], x4[z][:, 2 * u : 2 * u + 2, c0 : c0 + width])
-            if a < 2:
-                load_scales(6 * a, 6)
+            if a == 0:
+                offs_t = load_list(offs, "offs_t")
+                for i in range(3):
+                    nc.sync.dma_start(wsc_i[0:16, i], w_scales[i].rearrange("z q c -> q z c").bitcast(I32))
+            if a == 1:
+                for q in range(1, 4):
+                    nc.sync.dma_start(wsc_i[32 * q : 32 * q + 4], wsc_i[4 * q : 4 * q + 4])
 
-        wt = []
-        for i in range(3):
-            t = keep.tile([P, PASSES, N], U32, name="wt%d" % i, align_bytes=64)
-            nc.sync.dma_start(t[:].bitcast(I32), w_words[i].rearrange("z p n t -> p z (n t)").bitcast(I32))
-            wt.append(t)
+        wt = keep.tile([P, PASSES, 3, N], U32, name="wt", align_bytes=64)
+        for z in range(PASSES):
+            for i in range(3):
+                nc.sync.dma_start(wt[:, z, i, :].bitcast(I32), w_words[i][z].rearrange("p n t -> p (n t)").bitcast(I32))
         cen_t = load_list(cen, "cen_t")
         pos_t = [load_list(src, "pos%d_t" % d) for d, src in enumerate((pos1, pos2, pos3))]
 
@@ -133,13 +127,21 @@ def tile_picked_filmg_silu_e_kernel(
                 in_=woven[z][:, e0:e1, :].rearrange("p e u -> p (e u)").bitcast(BF16),
             )
 
-        acc = [[bank(2 * i + hf) for hf in range(2)] for i in range(3)]
+        spans = [
+            [(q * QUARTER, (q + 1) * QUARTER) for q in (0, 3, 1, 2)],
+            [(0, HALF), (HALF, S)],
+            [(0, HALF), (HALF, S)],
+        ]
+        acc = {}
+        for i in range(3):
+            for span in spans[i]:
+                acc[(i, span)] = bank(len(acc))
 
-        def product(i, z, hf):
-            cols = slice(hf * HALF, (hf + 1) * HALF)
+        def product(i, z, span):
+            cols = slice(span[0], span[1])
             nc.tensor.matmul_mx(
-                out=acc[i][hf][:],
-                lhsT=wt[i][:, z, :].bitcast(FP8X4),
+                out=acc[(i, span)][:, : span[1] - span[0]],
+                lhsT=wt[:, z, i, :].bitcast(FP8X4),
                 lhsT_scale=wsc[:, i, z, :],
                 rhs=codes[z][:, cols].bitcast(FP8X4),
                 rhs_scale=xsc[z][:, cols],
@@ -159,71 +161,74 @@ def tile_picked_filmg_silu_e_kernel(
         cast_pair(2)
         gather(2, 0, S)
         cast_pair(3)
-        for hf in range(2):
-            for i in range(3):
-                product(i, 0, hf)
-        nq = S // QUARTER
-        for q in range(nq + 2):
-            if q < nq:
-                gather(3, q * QUARTER, (q + 1) * QUARTER)
-                weave(1, q * QUARTER, (q + 1) * QUARTER, True)
-            if q >= 2:
-                quantize(1, (q - 2) * QUARTER, (q - 1) * QUARTER)
-        res = [keep.tile([P, S], F32, name="res%d" % i) for i in range(3)]
-        for hf in range(2):
-            for i in range(3):
-                product(i, 1, hf)
+        for i in range(3):
+            for span in spans[i]:
+                product(i, 0, span)
+        for e0, e1 in spans[0]:
+            gather(3, e0, e1)
+            weave(1, e0, e1, True)
+        quantize(1, 0, QUARTER)
+        quantize(1, S - QUARTER, S)
+        quantize(1, QUARTER, S - QUARTER)
+        res = [keep.tile([P, S], F32, name="res%d" % i)[:] for i in range(3)]
+        for i in range(3):
+            for span in spans[i]:
+                product(i, 1, span)
         g_sb, s_sb, h_sb = res
-        nc.scalar.copy(g_sb[:, :HALF], acc[0][0][:])
-        nc.vector.tensor_copy(g_sb[:, HALF:], acc[0][1][:])
-        for hf in range(2):
-            for i in (1, 2):
-                nc.scalar.copy(res[i][:, hf * HALF : (hf + 1) * HALF], acc[i][hf][:])
+        for i in range(3):
+            for span in spans[i]:
+                src = acc[(i, span)][:, : span[1] - span[0]]
+                if i == 0 and span[0] == HALF:
+                    nc.vector.tensor_copy(res[i][:, span[0] : span[1]], src)
+                else:
+                    nc.scalar.copy(res[i][:, span[0] : span[1]], src)
 
         gc_all = keep.tile([P, V], F32, name="gc_all")
         sc_all = keep.tile([P, V], F32, name="sc_all")
-        nc.vector.tensor_copy(gc_all[:], g_sb[:].indirect(cen_t[:]))
-        nc.vector.tensor_copy(sc_all[:], s_sb[:].indirect(cen_t[:]))
+        nc.vector.tensor_copy(gc_all[:], g_sb.indirect(cen_t[:]))
+        nc.vector.tensor_copy(sc_all[:], s_sb.indirect(cen_t[:]))
 
         def scaled(dst, d, v0, v1):
-            nc.vector.tensor_tensor(dst, h_sb[:].indirect(pos_t[d][:, v0 // 16 : v1 // 16]), gc_all[:, v0:v1], MULT)
+            nc.vector.tensor_tensor(dst, h_sb.indirect(pos_t[d][:, v0 // 16 : v1 // 16]), gc_all[:, v0:v1], MULT)
 
         sc = sc_all[:, :WIDE]
         prod = keep.tile([P, 3, WIDE], F32, name="prod_a")
         for d in range(3):
             scaled(prod[:, d, :], d, 0, WIDE)
         nblk = WIDE // P
-        act = keep.tile([P, 3, WIDE], F32, name="act_a", tag="act")
+        act = keep.tile([P, 3, WIDE], F32, name="act_a")
         o_sb = keep.tile([P, WIDE], F32, name="o_a")
-        ob = [bank(b) for b in range(nblk)]
+        blocks = [slice(b * P, (b + 1) * P) for b in range(nblk)]
+        ub = [bank(n) for n in range(3)]
+        ob = bank(3)
         for d in range(3):
-            if d < 2:
-                whole = bank(6 + d)
-                ub = [whole[:, b * P : (b + 1) * P] for b in range(nblk)]
-            else:
-                ub = [bank(3 + b)[:, :P] for b in range(nblk)]
-            for b in range(nblk):
-                blk = slice(b * P, (b + 1) * P)
-                nc.tensor.matmul(ub[b], sc[:, blk], ident[:], start=True, stop=False, is_transpose=True)
-                nc.tensor.matmul(ub[b], prod[:, d, blk], ident[:], start=False, stop=True, is_transpose=True)
-                if d == 2:
-                    nc.scalar.activation(act[:, d, blk], ub[b], SILU, bias=zero[:])
-            if d < 2:
-                nc.scalar.activation(act[:, d, :], whole[:, :WIDE], SILU, bias=zero[:])
-            for b in range(nblk):
-                blk = slice(b * P, (b + 1) * P)
-                nc.tensor.matmul(ob[b][:, :P], act[:, d, blk], ident[:], start=(d == 0), stop=(d == 2), is_transpose=True)
-        for b in range(nblk):
-            nc.scalar.copy(o_sb[:, b * P : (b + 1) * P], ob[b][:, :P])
+            for b, blk in enumerate(blocks):
+                nc.tensor.matmul(ub[d][:, blk], sc[:, blk], ident[:], start=(b == 0), stop=False, is_transpose=True)
+        for d in range(3):
+            for b, blk in enumerate(blocks):
+                nc.tensor.matmul(
+                    ub[d][:, blk], prod[:, d, blk], ident[:], start=False, stop=(b == nblk - 1), is_transpose=True
+                )
+            nc.scalar.activation(act[:, d, :], ub[d][:, :WIDE], SILU, bias=zero[:])
+            for b, blk in enumerate(blocks):
+                nc.tensor.matmul(
+                    ob[:, blk],
+                    act[:, d, blk],
+                    ident[:],
+                    start=(d == 0 and b == 0),
+                    stop=(d == 2 and b == nblk - 1),
+                    is_transpose=True,
+                )
+        nc.scalar.copy(o_sb[:], ob[:, :WIDE])
         nc.sync.dma_start(out[:, :WIDE], o_sb[:])
 
         rest = V - WIDE
         sc = sc_all[:, WIDE:]
+        pre = prod[:, 2, :].rearrange("p (d v) -> p d v", d=3)
         prod = keep.tile([P, 3, rest], F32, name="prod_b")
         scaled(prod[:, 0, :], 0, WIDE, V)
         scaled(prod[:, 1, :], 1, WIDE, V)
-        pre = keep.tile([P, 3, rest], F32, name="pre_b")
-        act = keep.tile([P, 3, rest], F32, name="act_b", tag="act")
+        act = keep.tile([P, 3, rest], F32, name="act_b")
         two = keep.tile([P, rest], F32, name="two_b")
         o_sb = keep.tile([P, rest], F32, name="o_b")
         nc.vector.tensor_tensor(pre[:, 0:2, :], prod[:, 0:2, :], sc.unsqueeze(1).to_broadcast([P, 2, rest]), ADD)

@@ -24,12 +24,12 @@ QUARTER = 256
 WIDE = 384
 
 PIECES = [
-    [(0, 2048, 1376)],
     [(1024, 1024, 0), (0, 1024, 688)],
-    [(1024, 1024, 0), (0, 1024, 496)],
+    [(1024, 1024, 0), (0, 512, 512), (512, 512, 344)],
+    [(1024, 1024, 0), (0, 1024, 400)],
     [(1536, 512, 0), (1024, 512, 0), (512, 512, 0), (0, 256, 256), (256, 256, 176)],
 ]
-LAP = 8
+LAPS = (520, 8, 264)
 
 
 def tile_picked_filmg_silu_e_kernel(
@@ -66,7 +66,7 @@ def tile_picked_filmg_silu_e_kernel(
         x4 = xT.rearrange("(z p j) t -> z p j t", z=PASSES, j=4)
         raw = [keep.tile([P, 2 * T], F32, name="raw%d" % a)[:].rearrange("p (u t) -> p u t", u=2) for a in range(4)]
         big = keep.tile([P, 5 * T], U32, name="big", align_bytes=64)
-        starts = [0, T - LAP, 3 * T - LAP, 4 * T - 2 * LAP]
+        starts = [0, T - LAPS[0], 3 * T - LAPS[1], 4 * T - LAPS[1] - LAPS[2]]
         pairs = [big[:, st : st + T] for st in starts]
         picked = [keep.tile([P, 2 * S], U32, name="picked%d" % z)[:].rearrange("p (u e) -> p u e", u=2) for z in range(PASSES)]
         woven1 = keep.tile([P, 2 * S], U32, name="woven1", align_bytes=64)
@@ -152,12 +152,12 @@ def tile_picked_filmg_silu_e_kernel(
         cast_pair(0)
         gather(0, 0, S)
         cast_pair(1)
-        gather(1, 0, HALF)
         gather(1, HALF, S)
-        weave(0, 0, HALF, False)
+        gather(1, 0, HALF)
         weave(0, HALF, S, False)
-        quantize(0, 0, HALF)
+        weave(0, 0, HALF, False)
         quantize(0, HALF, S)
+        quantize(0, 0, HALF)
         cast_pair(2)
         gather(2, 0, S)
         cast_pair(3)
@@ -167,9 +167,8 @@ def tile_picked_filmg_silu_e_kernel(
         for e0, e1 in spans[0]:
             gather(3, e0, e1)
             weave(1, e0, e1, True)
-        quantize(1, 0, QUARTER)
-        quantize(1, S - QUARTER, S)
-        quantize(1, QUARTER, S - QUARTER)
+        for e0, e1 in spans[0]:
+            quantize(1, e0, e1)
         res = [keep.tile([P, S], F32, name="res%d" % i)[:] for i in range(3)]
         for i in range(3):
             for span in spans[i]:
@@ -199,24 +198,29 @@ def tile_picked_filmg_silu_e_kernel(
         act = keep.tile([P, 3, WIDE], F32, name="act_a")
         o_sb = keep.tile([P, WIDE], F32, name="o_a")
         blocks = [slice(b * P, (b + 1) * P) for b in range(nblk)]
-        ub = [bank(n) for n in range(3)]
-        ob = bank(3)
+        ob = bank(2)
+        groups = [[(bank(d), blocks)] for d in range(2)] + [[(bank(3 + b), [blk]) for b, blk in enumerate(blocks)]]
         for d in range(3):
-            for b, blk in enumerate(blocks):
-                nc.tensor.matmul(ub[d][:, blk], sc[:, blk], ident[:], start=(b == 0), stop=False, is_transpose=True)
+            for ub, blks in groups[d]:
+                for blk in blks:
+                    nc.tensor.matmul(
+                        ub[:, blk], sc[:, blk], ident[:], start=(blk == blks[0]), stop=False, is_transpose=True
+                    )
         for d in range(3):
-            for b, blk in enumerate(blocks):
-                nc.tensor.matmul(
-                    ub[d][:, blk], prod[:, d, blk], ident[:], start=False, stop=(b == nblk - 1), is_transpose=True
-                )
-            nc.scalar.activation(act[:, d, :], ub[d][:, :WIDE], SILU, bias=zero[:])
-            for b, blk in enumerate(blocks):
+            for ub, blks in groups[d]:
+                for blk in blks:
+                    nc.tensor.matmul(
+                        ub[:, blk], prod[:, d, blk], ident[:], start=False, stop=(blk == blks[-1]), is_transpose=True
+                    )
+                cols = slice(blks[0].start, blks[-1].stop)
+                nc.scalar.activation(act[:, d, cols], ub[:, cols], SILU, bias=zero[:])
+            for blk in blocks:
                 nc.tensor.matmul(
                     ob[:, blk],
                     act[:, d, blk],
                     ident[:],
-                    start=(d == 0 and b == 0),
-                    stop=(d == 2 and b == nblk - 1),
+                    start=(d == 0 and blk == blocks[0]),
+                    stop=(d == 2 and blk == blocks[-1]),
                     is_transpose=True,
                 )
         nc.scalar.copy(o_sb[:], ob[:, :WIDE])

from contextlib import ExitStack

import concourse.mybir as mybir
from concourse.masks import make_identity

K, T, S, V, N = 1024, 2048, 1024, 512, 128
FLOPS = 3 * 2 * K * N * S

F32 = mybir.dt.float32
BF16 = mybir.dt.bfloat16
I32 = mybir.dt.int32
U32 = mybir.dt.uint32
U16 = mybir.dt.uint16
U8 = mybir.dt.uint8
FP8X4 = mybir.dt.float8_e4m3fn_x4
SILU = mybir.ActivationFunctionType.Silu
MULT = mybir.AluOpType.mult
ADD = mybir.AluOpType.add

P = 128
PASSES = 2
HALF = 512
QUARTER = 256
WIDE = 384

PIECES = [
    [(1024, 1024, 0), (0, 1024, 688)],
    [(1024, 1024, 0), (0, 512, 512), (512, 512, 344)],
    [(1024, 1024, 0), (0, 1024, 400)],
    [(1536, 512, 0), (1024, 512, 0), (512, 512, 0), (0, 256, 256), (256, 256, 176)],
]
LAPS = (520, 8, 264)


def tile_picked_filmg_silu_e_kernel(
    tc, xT, w1_words, w1_scales, w2_words, w2_scales, w3_words, w3_scales, offs, cen, pos1, pos2, pos3, out
):
    nc = tc.nc
    with ExitStack() as ctx:
        keep = ctx.enter_context(tc.tile_pool(name="keep", bufs=1))
        psum = ctx.enter_context(tc.psum_pool(name="psum", bufs=1))

        def load_list(src, name):
            t = keep.tile(list(src.shape), U16, name=name)
            nc.sync.dma_start(t[:], src)
            return t

        def bank(i):
            return psum.tile([P, HALF], F32, name="bank%d" % i, tag="bank%d" % i)

        w_words = [w1_words, w2_words, w3_words]
        w_scales = [w1_scales, w2_scales, w3_scales]

        wsc = keep.tile([P, 3, PASSES, N], U8, name="wsc", align_bytes=64)
        wsc_i = wsc[:].bitcast(I32)
        nc.vector.memset(wsc_i, 0)

        zero_in = keep.tile([P, 1], F32, name="zero_in")
        zero = keep.tile([P, 1], F32, name="zero")
        nc.vector.memset(zero_in[:], 0.0)
        nc.scalar.activation(zero[:], zero_in[:], SILU)

        ident = keep.tile([P, P], F32, name="ident")
        make_identity(nc, ident[:])

        x4 = xT.rearrange("(z p j) t -> z p j t", z=PASSES, j=4)
        raw = [keep.tile([P, 2 * T], F32, name="raw%d" % a)[:].rearrange("p (u t) -> p u t", u=2) for a in range(4)]
        big = keep.tile([P, 5 * T], U32, name="big", align_bytes=64)
        starts = [0, T - LAPS[0], 3 * T - LAPS[1], 4 * T - LAPS[1] - LAPS[2]]
        pairs = [big[:, st : st + T] for st in starts]
        picked = [keep.tile([P, 2 * S], U32, name="picked%d" % z)[:].rearrange("p (u e) -> p u e", u=2) for z in range(PASSES)]
        woven1 = keep.tile([P, 2 * S], U32, name="woven1", align_bytes=64)
        woven = [w.rearrange("p (e u) -> p e u", u=2) for w in (big[:, 2 * T : 3 * T], woven1[:])]
        codes = [keep.tile([P, S], U32, name="codes%d" % z, align_bytes=64) for z in range(PASSES)]
        xsc = [keep.tile([P, S], U8, name="xsc%d" % z, align_bytes=64) for z in range(PASSES)]

        for a in range(4):
            z, u = divmod(a, 2)
            for c0, width, share in PIECES[a]:
                nc.sync.dma_start(raw[a][:, :, c0 : c0 + width], x4[z][:, 2 * u : 2 * u + 2, c0 : c0 + width])
            if a == 0:
                offs_t = load_list(offs, "offs_t")
                for i in range(3):
                    nc.sync.dma_start(wsc_i[0:16, i], w_scales[i].rearrange("z q c -> q z c").bitcast(I32))
            if a == 1:
                for q in range(1, 4):
                    nc.sync.dma_start(wsc_i[32 * q : 32 * q + 4], wsc_i[4 * q : 4 * q + 4])

        wt = keep.tile([P, PASSES, 3, N], U32, name="wt", align_bytes=64)
        for z in range(PASSES):
            for i in range(3):
                nc.sync.dma_start(wt[:, z, i, :].bitcast(I32), w_words[i][z].rearrange("p n t -> p (n t)").bitcast(I32))
        cen_t = load_list(cen, "cen_t")
        pos_t = [load_list(src, "pos%d_t" % d) for d, src in enumerate((pos1, pos2, pos3))]

        def cast(a, c0, c1, on_scalar):
            dst = pairs[a][:, c0:c1].bitcast(BF16).rearrange("p (t u) -> p t u", u=2)
            src = raw[a][:, :, c0:c1].rearrange("p u t -> p t u")
            if on_scalar:
                nc.scalar.copy(dst, src)
            else:
                nc.vector.tensor_copy(dst, src)

        def cast_pair(a):
            for c0, width, share in PIECES[a]:
                if share > 0:
                    cast(a, c0, c0 + share, False)
                if share < width:
                    cast(a, c0 + share, c0 + width, True)

        def gather(a, e0, e1):
            z, u = divmod(a, 2)
            nc.vector.tensor_copy(picked[z][:, u, e0:e1], pairs[a].indirect(offs_t[:, e0 // 16 : e1 // 16]))

        def weave(z, e0, e1, on_scalar):
            src = picked[z][:, :, e0:e1].rearrange("p u e -> p e u")
            dst = woven[z][:, e0:e1, :]
            if on_scalar:
                nc.scalar.copy(dst, src)
            else:
                nc.vector.tensor_copy(dst.bitcast(I32), picked[z][:, :, e0:e1].bitcast(I32).rearrange("p u e -> p e u"))

        def quantize(z, e0, e1):
            nc.vector.quantize_mx(
                out=codes[z][:, e0:e1].bitcast(FP8X4),
                scales=xsc[z][:, e0:e1],
                in_=woven[z][:, e0:e1, :].rearrange("p e u -> p (e u)").bitcast(BF16),
            )

        spans = [
            [(q * QUARTER, (q + 1) * QUARTER) for q in (0, 3, 1, 2)],
            [(0, HALF), (HALF, S)],
            [(0, HALF), (HALF, S)],
        ]
        acc = {}
        for i in range(3):
            for span in spans[i]:
                acc[(i, span)] = bank(len(acc))

        def product(i, z, span):
            cols = slice(span[0], span[1])
            nc.tensor.matmul_mx(
                out=acc[(i, span)][:, : span[1] - span[0]],
                lhsT=wt[:, z, i, :].bitcast(FP8X4),
                lhsT_scale=wsc[:, i, z, :],
                rhs=codes[z][:, cols].bitcast(FP8X4),
                rhs_scale=xsc[z][:, cols],
                start=(z == 0),
                stop=(z == PASSES - 1),
            )

        cast_pair(0)
        gather(0, 0, S)
        cast_pair(1)
        gather(1, HALF, S)
        gather(1, 0, HALF)
        weave(0, HALF, S, False)
        weave(0, 0, HALF, False)
        quantize(0, HALF, S)
        quantize(0, 0, HALF)
        cast_pair(2)
        gather(2, 0, S)
        cast_pair(3)
        for i in range(3):
            for span in spans[i]:
                product(i, 0, span)
        for e0, e1 in spans[0]:
            gather(3, e0, e1)
            weave(1, e0, e1, True)
        for e0, e1 in spans[0]:
            quantize(1, e0, e1)
        res = [keep.tile([P, S], F32, name="res%d" % i)[:] for i in range(3)]
        for i in range(3):
            for span in spans[i]:
                product(i, 1, span)
        g_sb, s_sb, h_sb = res
        for i in range(3):
            for span in spans[i]:
                src = acc[(i, span)][:, : span[1] - span[0]]
                if i == 0 and span[0] == HALF:
                    nc.vector.tensor_copy(res[i][:, span[0] : span[1]], src)
                else:
                    nc.scalar.copy(res[i][:, span[0] : span[1]], src)

        gc_all = keep.tile([P, V], F32, name="gc_all")
        sc_all = keep.tile([P, V], F32, name="sc_all")
        nc.vector.tensor_copy(gc_all[:], g_sb.indirect(cen_t[:]))
        nc.vector.tensor_copy(sc_all[:], s_sb.indirect(cen_t[:]))

        def scaled(dst, d, v0, v1):
            nc.vector.tensor_tensor(dst, h_sb.indirect(pos_t[d][:, v0 // 16 : v1 // 16]), gc_all[:, v0:v1], MULT)

        sc = sc_all[:, :WIDE]
        prod = keep.tile([P, 3, WIDE], F32, name="prod_a")
        for d in range(3):
            scaled(prod[:, d, :], d, 0, WIDE)
        nblk = WIDE // P
        act = keep.tile([P, 3, WIDE], F32, name="act_a")
        o_sb = keep.tile([P, WIDE], F32, name="o_a")
        blocks = [slice(b * P, (b + 1) * P) for b in range(nblk)]
        ob = bank(2)
        groups = [[(bank(d), blocks)] for d in range(2)] + [[(bank(3 + b), [blk]) for b, blk in enumerate(blocks)]]
        for d in range(3):
            for ub, blks in groups[d]:
                for blk in blks:
                    nc.tensor.matmul(
                        ub[:, blk], sc[:, blk], ident[:], start=(blk == blks[0]), stop=False, is_transpose=True
                    )
        for d in range(3):
            for ub, blks in groups[d]:
                for blk in blks:
                    nc.tensor.matmul(
                        ub[:, blk], prod[:, d, blk], ident[:], start=False, stop=(blk == blks[-1]), is_transpose=True
                    )
                cols = slice(blks[0].start, blks[-1].stop)
                nc.scalar.activation(act[:, d, cols], ub[:, cols], SILU, bias=zero[:])
            for blk in blocks:
                nc.tensor.matmul(
                    ob[:, blk],
                    act[:, d, blk],
                    ident[:],
                    start=(d == 0 and blk == blocks[0]),
                    stop=(d == 2 and blk == blocks[-1]),
                    is_transpose=True,
                )
        nc.scalar.copy(o_sb[:], ob[:, :WIDE])
        nc.sync.dma_start(out[:, :WIDE], o_sb[:])

        rest = V - WIDE
        sc = sc_all[:, WIDE:]
        pre = prod[:, 2, :].rearrange("p (d v) -> p d v", d=3)
        prod = keep.tile([P, 3, rest], F32, name="prod_b")
        scaled(prod[:, 0, :], 0, WIDE, V)
        scaled(prod[:, 1, :], 1, WIDE, V)
        act = keep.tile([P, 3, rest], F32, name="act_b")
        two = keep.tile([P, rest], F32, name="two_b")
        o_sb = keep.tile([P, rest], F32, name="o_b")
        nc.vector.tensor_tensor(pre[:, 0:2, :], prod[:, 0:2, :], sc.unsqueeze(1).to_broadcast([P, 2, rest]), ADD)
        nc.scalar.activation(act[:, 0:2, :], pre[:, 0:2, :], SILU, bias=zero[:])
        scaled(prod[:, 2, :], 2, WIDE, V)
        nc.vector.tensor_tensor(pre[:, 2, :], prod[:, 2, :], sc, ADD)
        nc.scalar.activation(act[:, 2, :], pre[:, 2, :], SILU, bias=zero[:])
        nc.vector.tensor_tensor(two[:], act[:, 0, :], act[:, 1, :], ADD)
        nc.vector.tensor_tensor(o_sb[:], two[:], act[:, 2, :], ADD)
        nc.sync.dma_start(out[:, WIDE:], o_sb[:])
